import numpy as np, ml_dtypes
CORES = [14,30,46,142,158,174,270,286,302,398,414,430]
N = 12
def setup_inputs(rng):
    dy = rng.standard_normal((N, 128, N * 128), dtype=np.float32).astype(ml_dtypes.bfloat16)
    dyt = np.concatenate([dy[:, :, 128 * j:128 * j + 128].transpose(0, 2, 1) for j in range(N)], axis=2)
    return {"x": rng.standard_normal((N, 128, 128), dtype=np.float32).astype(ml_dtypes.bfloat16), "wt": rng.standard_normal((N, 128, 128), dtype=np.float32).astype(ml_dtypes.bfloat16), "dy": dy, "dyt": dyt}
def setup_inputs_big(rng):
    d = setup_inputs(rng)
    for k in ("x", "wt", "dy", "dyt"): d[k] = (d[k].astype(np.float32) * 1024.0).astype(d[k].dtype)
    return d
def setup_inputs_small(rng):
    d = setup_inputs(rng)
    for k in ("x", "wt", "dy", "dyt"): d[k] = (d[k].astype(np.float32) * (1 / 1024.0)).astype(d[k].dtype)
    return d
def setup_inputs_apart(rng):
    d = setup_inputs(rng)
    f = (10.0 ** rng.permutation(np.linspace(-1.5, 1.5, N))).astype(np.float32).reshape(N, 1, 1)
    for k in ("x", "wt", "dy", "dyt"): d[k] = (d[k].astype(np.float32) * f).astype(d[k].dtype)
    return d
def reference(x, wt, dy, dyt):
    X, WT, DY, DYT = x.astype(np.float64), wt.astype(np.float64), dy.astype(np.float64), dyt.astype(np.float64)
    dx = np.zeros((N, 128, 128)); dw = np.zeros((N, 128, 128))
    for r in range(N):
        for j in range(N):
            dx[r] += WT[j].T @ DY[j][:, 128 * r:128 * r + 128]
            dw[r] += X[j].T @ DYT[r][:, 128 * j:128 * j + 128]
    return {"dx": dx.astype(ml_dtypes.bfloat16), "dw": dw.astype(ml_dtypes.bfloat16)}

@@ -1,0 +1,178 @@
+from concourse.bass import DstId, RemoteDMATransfer
+from concourse.mybir import AluOpType
+
+B = 128
+N = 12
+G = 6
+
+O_AT, P_AT = (0, 5, 8), (1, 4, 9)
+WINDOW = {1: (0, 0, 1, 2), 2: (3, 2, 1, 0), 3: (4, 1, 0, 2), 4: (7, 1, 2, 0), 5: (8, 0, 1, 2)}
+PLAN = (((1, 8),), ((2, 4), (3, 4)), ((4, 4), (5, 4)))
+ENGINES_OF = {s: n for call in PLAN for s, n in call}
+
+SCRATCH = {
+    "win": ("sbuf", [128, 11 * B], "bfloat16"),
+    "wts": ("sbuf", [128, B], "bfloat16"),
+    "dys": ("sbuf", [128, N * B], "bfloat16"),
+    "dyts": ("sbuf", [128, N * B], "bfloat16"),
+    "pack": ("sbuf", [128, G * B], "bfloat16"),
+    "land": ("sbuf", [128, G * B], "bfloat16"),
+    "rx": ("sbuf", [128, 15 * B], "bfloat16"),
+    "dxs": ("sbuf", [128, B], "bfloat16"),
+    "dws": ("sbuf", [128, B], "bfloat16"),
+    "ps0": ("psum", [128, 512], "float32"),
+    "ps1": ("psum", [128, 512], "float32"),
+    "ps2": ("psum", [128, 512], "float32"),
+    "ps3": ("psum", [128, 512], "float32"),
+    "psw": ("psum", [128, 512], "float32"),
+}
+SEMAPHORES = ["lx0", "ocp", "lwt", "ldo", "ldm", "ldt",
+              "mm0", "mm1", "mm2", "mm3", "mmw",
+              "cp", "pcp", "s12", "s34", "s5", "acc", "dwc",
+              "xarr", "parr", "arr1", "arr2", "arr3", "arr4", "arr5", "sent", "stx", "stw"]
+
+
+def blk(t, a, n=1):
+    return t[:, a * B:(a + n) * B]
+
+
+def rank_program(g, core, T, topo):
+    r = T.rank_of(core)
+    if r is None:
+        return
+    cores, S = T.cores, T.sem
+    sy, sc, pe, ve = g.sync, g.scalar, g.tensor, g.vector
+
+    def ring_of(q):
+        return sorted([q] + [k for k in range(N) if topo.same_plane(cores[q], cores[k])])
+
+    def order_of(q):
+        ring = ring_of(q)
+        s = ring.index(q)
+        return [ring[(s + i) % G] for i in range(1, G)] + [q]
+
+    def partner_of(q):
+        return [k for k in range(N) if topo.rack(topo.host(cores[k])) != topo.rack(topo.host(cores[q]))
+                and topo.chip(cores[k]) == topo.chip(cores[q]) and topo.may_write(cores[q], cores[k])][0]
+
+    def engines(dst):
+        m = topo.mask(core, dst)
+        return [e for e in range(16) if (m >> e) & 1]
+
+    def bits(es):
+        return sum(1 << e for e in es)
+
+    mine = order_of(r)
+    pr = partner_of(r)
+    theirs = order_of(pr)
+    ring = ring_of(r)
+    pos = ring.index(r)
+
+    far, near = sorted(theirs), sorted(mine)
+    sy.dma_start(blk(T.win, O_AT[0]), T.x[:]).then_inc(S.lx0, 16)
+    sc.dma_start(blk(T.dys, far[0], G), blk(T.dy, far[0], G)).then_inc(S.ldo, 16)
+    sy.dma_start(T.wts[:], T.wt[:]).then_inc(S.lwt, 16)
+    sy.dma_start(blk(T.dys, near[0], G), blk(T.dy, near[0], G)).then_inc(S.ldm, 16)
+    sy.dma_start(T.dyts[:], T.dyt[:]).then_inc(S.ldt, 16)
+
+    def partials(ks, bank, sem):
+        runs = []
+        for at, k in enumerate(ks):
+            if runs and runs[-1][1] + runs[-1][2] == k:
+                runs[-1][2] += 1
+            else:
+                runs.append([at, k, 1])
+        for at, k, n in runs:
+            pe.matmul(blk(bank, at, n), T.wts[:], blk(T.dys, k, n), True, True).then_inc(sem, 1)
+        return len(runs)
+
+    pe.wait_ge(S.lwt, 16)
+    pe.wait_ge(S.ldo, 16)
+    n0 = partials(theirs[0:3], T.ps0, S.mm0)
+    n1 = partials(theirs[3:6], T.ps1, S.mm1)
+    pe.wait_ge(S.ldm, 16)
+    n2 = partials(mine[0:4], T.ps2, S.mm2)
+    n3 = partials(mine[4:6], T.ps3, S.mm3)
+    dwp = blk(T.psw, 0)
+    pe.wait_ge(S.lx0, 16)
+    pe.wait_ge(S.ldt, 16)
+    pe.matmul(dwp, blk(T.win, O_AT[0]), blk(T.dyts, r), True, False)
+    pe.wait_ge(S.xarr, 8)
+    pe.matmul(dwp, blk(T.win, P_AT[0]), blk(T.dyts, pr), False, False)
+    for i in range(1, G):
+        src = ring[(pos - i) % G]
+        o, p = WINDOW[i][1], WINDOW[i][2]
+        pe.wait_ge(S["arr%d" % i], ENGINES_OF[i])
+        pe.matmul(dwp, blk(T.rx, 3 * (i - 1) + o), blk(T.dyts, src), False, False)
+        if i < G - 1:
+            pe.matmul(dwp, blk(T.rx, 3 * (i - 1) + p), blk(T.dyts, partner_of(src)), False, False)
+        else:
+            pe.matmul(dwp, blk(T.rx, 3 * (i - 1) + p), blk(T.dyts, partner_of(src)), False, True).then_inc(S.mmw, 1)
+
+    add = AluOpType.add
+    ve.wait_ge(S.lx0, 16)
+    ve.tensor_copy(blk(T.win, O_AT[1]), blk(T.win, O_AT[0])).then_inc(S.ocp, 1)
+    ve.tensor_copy(blk(T.win, O_AT[2]), blk(T.win, O_AT[0])).then_inc(S.ocp, 1)
+    ve.wait_ge(S.mm0, n0)
+    ve.tensor_copy(blk(T.pack, 0, 3), blk(T.ps0, 0, 3)).then_inc(S.cp, 1)
+    ve.wait_ge(S.mm1, n1)
+    ve.tensor_copy(blk(T.pack, 3, 3), blk(T.ps1, 0, 3)).then_inc(S.cp, 1)
+    ve.wait_ge(S.xarr, 8)
+    ve.tensor_copy(blk(T.win, P_AT[1]), blk(T.win, P_AT[0])).then_inc(S.pcp, 1)
+    ve.tensor_copy(blk(T.win, P_AT[2]), blk(T.win, P_AT[0])).then_inc(S.pcp, 1)
+    ve.wait_ge(S.mm2, n2)
+    ve.wait_ge(S.parr, 8)
+    ve.tensor_tensor(blk(T.win, 2, 2), blk(T.ps2, 0, 2), blk(T.land, 0, 2), add).then_inc(S.s12, 1)
+    ve.tensor_tensor(blk(T.win, 6, 2), blk(T.ps2, 2, 2), blk(T.land, 2, 2), add).then_inc(S.s34, 1)
+    ve.wait_ge(S.mm3, n3)
+    ve.tensor_tensor(blk(T.win, 10), blk(T.ps3, 0), blk(T.land, 4), add).then_inc(S.s5, 1)
+    acc = blk(T.ps3, 1)
+    ve.tensor_tensor(acc, acc, blk(T.land, 5), add).then_inc(S.acc, 1)
+    for i in range(1, G):
+        ve.wait_ge(S["arr%d" % i], ENGINES_OF[i])
+        ve.wait_ge(S.acc, i)
+        out = acc if i < G - 1 else T.dxs[:]
+        ve.tensor_tensor(out, acc, blk(T.rx, 3 * (i - 1) + WINDOW[i][3]), add).then_inc(S.acc, 1)
+    ve.wait_ge(S.mmw, 1)
+    ve.tensor_copy(T.dws[:], dwp).then_inc(S.dwc, 1)
+
+    sy.wait_ge(S.acc, G)
+    sy.dma_start(T.dx[:], T.dxs[:]).then_inc(S.stx, 16)
+    sc.wait_ge(S.dwc, 1)
+    sc.dma_start(T.dw[:], T.dws[:]).then_inc(S.stw, 16)
+
+    pc = cores[pr]
+    rid, pid = topo.addr(pc, core)
+    cable = bits(engines(pc))
+    g.wait_ge(S.lx0, 16)
+    g.remote_dma(out_ap=blk(T.win, P_AT[0]), in_ap=blk(T.win, O_AT[0]), remote_sem=S.xarr, local_sem=S.sent,
+                 pid=pid, routing_id=rid, dma_engine_mask=cable)
+    g.wait_ge(S.cp, 2)
+    g.remote_dma(out_ap=T.land[:], in_ap=T.pack[:], remote_sem=S.parr, local_sem=S.sent,
+                 pid=pid, routing_id=rid, dma_engine_mask=cable)
+    sent = 16
+    needs = {1: ("s12",), 2: ("s12", "pcp", "ocp"), 3: ("s34", "pcp", "ocp"), 4: ("s34", "pcp", "ocp"), 5: ("s5", "pcp", "ocp")}
+    full = {"s12": 1, "s34": 1, "s5": 1, "pcp": 2, "ocp": 2}
+    g.wait_ge(S.xarr, 8)
+    waited = []
+    for call in PLAN:
+        for s, n in call:
+            for name in needs[s]:
+                if name not in waited:
+                    waited.append(name)
+                    g.wait_ge(S[name], full[name])
+        used = 0
+        trs = []
+        for s, n in call:
+            d = cores[mine[s - 1]]
+            es = engines(d)[used:used + n]
+            used += n
+            drid, dpid = topo.addr(d, core)
+            trs.append(RemoteDMATransfer(dst_ids=[DstId(rid=drid, pnc=dpid)], dma_engine_mask=bits(es),
+                                         remote_sem=S["arr%d" % s], src=blk(T.win, WINDOW[s][0], 3),
+                                         dst=blk(T.rx, 3 * (s - 1), 3)))
+            sent += n
+        g.remote_dma_fused(trs, local_sem=S.sent)
+    g.wait_ge(S.sent, sent)
+    g.wait_ge(S.stx, 16)
+    g.wait_ge(S.stw, 16)

@@ -26,10 +26,10 @@ SCRATCH = {
     "ps3": ("psum", [128, 512], "float32"),
     "psw": ("psum", [128, 512], "float32"),
 }
-SEMAPHORES = ["lx0", "ocp", "lwt", "ldo", "ldm", "ldt",
+SEMAPHORES = ["lx0", "ocp", "lwt", "lda", "ldb", "ldm", "ldt",
               "mm0", "mm1", "mm2", "mm3", "mmw",
-              "cp", "pcp", "s12", "s34", "s5", "acc", "dwc",
-              "xarr", "parr", "arr1", "arr2", "arr3", "arr4", "arr5", "sent", "stx", "stw"]
+              "cpa", "cpb", "pcp", "s1", "s2", "s3", "s4", "s5", "acc", "dwc",
+              "xarr", "pa", "pb", "arr1", "arr2", "arr3", "arr4", "arr5", "sent", "stx", "stw"]
 
 
 def blk(t, a, n=1):
@@ -62,33 +62,40 @@ def rank_program(g, core, T, topo):
     def bits(es):
         return sum(1 << e for e in es)
 
-    mine = order_of(r)
-    pr = partner_of(r)
-    theirs = order_of(pr)
-    ring = ring_of(r)
-    pos = ring.index(r)
-
-    far, near = sorted(theirs), sorted(mine)
-    sy.dma_start(blk(T.win, O_AT[0]), T.x[:]).then_inc(S.lx0, 16)
-    sc.dma_start(blk(T.dys, far[0], G), blk(T.dy, far[0], G)).then_inc(S.ldo, 16)
-    sy.dma_start(T.wts[:], T.wt[:]).then_inc(S.lwt, 16)
-    sy.dma_start(blk(T.dys, near[0], G), blk(T.dy, near[0], G)).then_inc(S.ldm, 16)
-    sy.dma_start(T.dyts[:], T.dyt[:]).then_inc(S.ldt, 16)
-
-    def partials(ks, bank, sem):
+    def runs_of(ks):
         runs = []
         for at, k in enumerate(ks):
             if runs and runs[-1][1] + runs[-1][2] == k:
                 runs[-1][2] += 1
             else:
                 runs.append([at, k, 1])
-        for at, k, n in runs:
+        return runs
+
+    mine = order_of(r)
+    pr = partner_of(r)
+    theirs = order_of(pr)
+    ring = ring_of(r)
+    pos = ring.index(r)
+
+    near = sorted(mine)
+    sy.dma_start(blk(T.win, O_AT[0]), T.x[:]).then_inc(S.lx0, 16)
+    for at, k, n in runs_of(theirs[0:3]):
+        sc.dma_start(blk(T.dys, k, n), blk(T.dy, k, n)).then_inc(S.lda, 16)
+    sy.dma_start(T.wts[:], T.wt[:]).then_inc(S.lwt, 16)
+    for at, k, n in runs_of(theirs[3:6]):
+        sc.dma_start(blk(T.dys, k, n), blk(T.dy, k, n)).then_inc(S.ldb, 16)
+    sy.dma_start(blk(T.dys, near[0], G), blk(T.dy, near[0], G)).then_inc(S.ldm, 16)
+    sy.dma_start(T.dyts[:], T.dyt[:]).then_inc(S.ldt, 16)
+
+    def partials(ks, bank, sem):
+        for at, k, n in runs_of(ks):
             pe.matmul(blk(bank, at, n), T.wts[:], blk(T.dys, k, n), True, True).then_inc(sem, 1)
-        return len(runs)
+        return len(runs_of(ks))
 
     pe.wait_ge(S.lwt, 16)
-    pe.wait_ge(S.ldo, 16)
+    pe.wait_ge(S.lda, 16 * len(runs_of(theirs[0:3])))
     n0 = partials(theirs[0:3], T.ps0, S.mm0)
+    pe.wait_ge(S.ldb, 16 * len(runs_of(theirs[3:6])))
     n1 = partials(theirs[3:6], T.ps1, S.mm1)
     pe.wait_ge(S.ldm, 16)
     n2 = partials(mine[0:4], T.ps2, S.mm2)
@@ -114,16 +121,19 @@ def rank_program(g, core, T, topo):
     ve.tensor_copy(blk(T.win, O_AT[1]), blk(T.win, O_AT[0])).then_inc(S.ocp, 1)
     ve.tensor_copy(blk(T.win, O_AT[2]), blk(T.win, O_AT[0])).then_inc(S.ocp, 1)
     ve.wait_ge(S.mm0, n0)
-    ve.tensor_copy(blk(T.pack, 0, 3), blk(T.ps0, 0, 3)).then_inc(S.cp, 1)
+    ve.tensor_copy(blk(T.pack, 0, 3), blk(T.ps0, 0, 3)).then_inc(S.cpa, 1)
     ve.wait_ge(S.mm1, n1)
-    ve.tensor_copy(blk(T.pack, 3, 3), blk(T.ps1, 0, 3)).then_inc(S.cp, 1)
+    ve.tensor_copy(blk(T.pack, 3, 3), blk(T.ps1, 0, 3)).then_inc(S.cpb, 1)
     ve.wait_ge(S.xarr, 8)
     ve.tensor_copy(blk(T.win, P_AT[1]), blk(T.win, P_AT[0])).then_inc(S.pcp, 1)
     ve.tensor_copy(blk(T.win, P_AT[2]), blk(T.win, P_AT[0])).then_inc(S.pcp, 1)
     ve.wait_ge(S.mm2, n2)
-    ve.wait_ge(S.parr, 8)
-    ve.tensor_tensor(blk(T.win, 2, 2), blk(T.ps2, 0, 2), blk(T.land, 0, 2), add).then_inc(S.s12, 1)
-    ve.tensor_tensor(blk(T.win, 6, 2), blk(T.ps2, 2, 2), blk(T.land, 2, 2), add).then_inc(S.s34, 1)
+    ve.wait_ge(S.pa, 8)
+    ve.tensor_tensor(blk(T.win, 2), blk(T.ps2, 0), blk(T.land, 0), add).then_inc(S.s1, 1)
+    ve.tensor_tensor(blk(T.win, 3), blk(T.ps2, 1), blk(T.land, 1), add).then_inc(S.s2, 1)
+    ve.tensor_tensor(blk(T.win, 6), blk(T.ps2, 2), blk(T.land, 2), add).then_inc(S.s3, 1)
+    ve.wait_ge(S.pb, 8)
+    ve.tensor_tensor(blk(T.win, 7), blk(T.ps2, 3), blk(T.land, 3), add).then_inc(S.s4, 1)
     ve.wait_ge(S.mm3, n3)
     ve.tensor_tensor(blk(T.win, 10), blk(T.ps3, 0), blk(T.land, 4), add).then_inc(S.s5, 1)
     acc = blk(T.ps3, 1)
@@ -147,12 +157,15 @@ def rank_program(g, core, T, topo):
     g.wait_ge(S.lx0, 16)
     g.remote_dma(out_ap=blk(T.win, P_AT[0]), in_ap=blk(T.win, O_AT[0]), remote_sem=S.xarr, local_sem=S.sent,
                  pid=pid, routing_id=rid, dma_engine_mask=cable)
-    g.wait_ge(S.cp, 2)
-    g.remote_dma(out_ap=T.land[:], in_ap=T.pack[:], remote_sem=S.parr, local_sem=S.sent,
+    g.wait_ge(S.cpa, 1)
+    g.remote_dma(out_ap=blk(T.land, 0, 3), in_ap=blk(T.pack, 0, 3), remote_sem=S.pa, local_sem=S.sent,
                  pid=pid, routing_id=rid, dma_engine_mask=cable)
-    sent = 16
-    needs = {1: ("s12",), 2: ("s12", "pcp", "ocp"), 3: ("s34", "pcp", "ocp"), 4: ("s34", "pcp", "ocp"), 5: ("s5", "pcp", "ocp")}
-    full = {"s12": 1, "s34": 1, "s5": 1, "pcp": 2, "ocp": 2}
+    g.wait_ge(S.cpb, 1)
+    g.remote_dma(out_ap=blk(T.land, 3, 3), in_ap=blk(T.pack, 3, 3), remote_sem=S.pb, local_sem=S.sent,
+                 pid=pid, routing_id=rid, dma_engine_mask=cable)
+    sent = 24
+    needs = {1: ("s1",), 2: ("s2", "pcp", "ocp"), 3: ("s3", "pcp", "ocp"), 4: ("s4", "pcp", "ocp"), 5: ("s5", "pcp", "ocp")}
+    full = {"s1": 1, "s2": 1, "s3": 1, "s4": 1, "s5": 1, "pcp": 2, "ocp": 2}
     g.wait_ge(S.xarr, 8)
     waited = []
     for call in PLAN:

@@ -1,23 +1,24 @@
 from concourse.bass import DstId, RemoteDMATransfer
-from concourse.mybir import AluOpType
+from concourse.mybir import AluOpType, ActivationFunctionType
 
 B = 128
 N = 12
 G = 6
-
-O_AT, P_AT = (0, 5, 8), (1, 4, 9)
-WINDOW = {1: (0, 0, 1, 2), 2: (3, 2, 1, 0), 3: (4, 1, 0, 2), 4: (7, 1, 2, 0), 5: (8, 0, 1, 2)}
-PLAN = (((1, 8),), ((2, 4), (3, 4)), ((4, 4), (5, 4)))
-ENGINES_OF = {s: n for call in PLAN for s, n in call}
+WORLD = 512
 
 SCRATCH = {
-    "win": ("sbuf", [128, 11 * B], "bfloat16"),
+    "hb": ("sbuf", [128, 5 * B], "bfloat16"),
+    "hs": ("sbuf", [128, 4 * B], "bfloat16"),
+    "hl": ("sbuf", [128, 2 * B], "bfloat16"),
     "wts": ("sbuf", [128, B], "bfloat16"),
     "dys": ("sbuf", [128, N * B], "bfloat16"),
     "dyts": ("sbuf", [128, N * B], "bfloat16"),
-    "pack": ("sbuf", [128, G * B], "bfloat16"),
-    "land": ("sbuf", [128, G * B], "bfloat16"),
-    "rx": ("sbuf", [128, 15 * B], "bfloat16"),
+    "stg": ("sbuf", [128, 8 * B], "bfloat16"),
+    "pack": ("sbuf", [128, 3 * B], "bfloat16"),
+    "rxw": ("sbuf", [128, 3 * G * B], "bfloat16"),
+    "rxm": ("sbuf", [128, 3 * B], "bfloat16"),
+    "ones": ("sbuf", [128, B], "bfloat16"),
+    "idn": ("sbuf", [128, B], "bfloat16"),
     "dxs": ("sbuf", [128, B], "bfloat16"),
     "dws": ("sbuf", [128, B], "bfloat16"),
     "ps0": ("psum", [128, 512], "float32"),
@@ -25,35 +26,61 @@ SCRATCH = {
     "ps2": ("psum", [128, 512], "float32"),
     "ps3": ("psum", [128, 512], "float32"),
     "psw": ("psum", [128, 512], "float32"),
+    "pt0": ("psum", [128, 512], "float32"),
+    "pt1": ("psum", [128, 512], "float32"),
+    "pt2": ("psum", [128, 512], "float32"),
 }
-SEMAPHORES = ["lx0", "ocp", "lwt", "lda", "ldb", "ldm", "ldt",
-              "mm0", "mm1", "mm2", "mm3", "mmw",
-              "cpa", "cpb", "pcp", "s1", "s2", "s3", "s4", "s5", "acc", "dwc",
-              "xarr", "pa", "pb", "arr1", "arr2", "arr3", "arr4", "arr5", "sent", "stx", "stw"]
+SEMAPHORES = ["lx", "lwt", "lf0", "lf1", "lf2", "ln", "one", "idy",
+              "mm0", "mm1", "mm2", "mmr", "mmw", "tp0", "tp1", "tp2", "tc0", "tc1", "tc2",
+              "xcp", "cs0", "cs1", "cp2", "s5", "ocp", "sa", "sb", "acc", "dwc",
+              "ho", "hst", "hpx", "hp", "w0", "w1", "w2", "w3", "w4", "w5", "wm", "sent", "stx", "stw"]
+
+PLANS = {}
 
 
 def blk(t, a, n=1):
     return t[:, a * B:(a + n) * B]
 
 
+def runs_of(ks):
+    runs = []
+    for k in sorted(ks):
+        if runs and runs[-1][0] + runs[-1][1] == k:
+            runs[-1][1] += 1
+        else:
+            runs.append([k, 1])
+    return runs
+
+
+def make_plan(T, topo):
+    if "p" in PLANS:
+        return PLANS["p"]
+    cores = list(T.cores)
+    ring, partner, units, helpers, role = {}, {}, {}, {}, {}
+    for q in range(N):
+        ring[q] = sorted([q] + [k for k in range(N) if topo.same_plane(cores[q], cores[k])])
+        partner[q] = [k for k in range(N) if topo.rack(topo.host(cores[k])) != topo.rack(topo.host(cores[q]))
+                      and topo.chip(cores[k]) == topo.chip(cores[q]) and topo.may_write(cores[q], cores[k])][0]
+    for q in range(N):
+        rg = ring[q]
+        gq = rg.index(q) // 2
+        pairs = [[rg[2 * i], rg[2 * i + 1]] for i in range(G // 2)]
+        mate = [k for k in pairs[gq] if k != q][0]
+        units[q] = [pairs[(gq + 1) % 3], pairs[(gq + 2) % 3], [mate, q]]
+        c = cores[q]
+        free = [h for h in range(WORLD) if h not in cores and topo.host(h) == topo.host(c) and topo.chip(h) == topo.chip(c)
+                and all(topo.may_write(h, cores[k]) for k in rg if k != q)]
+        helpers[q] = [[h for h in free if topo.die(h) != topo.die(c)][0], [h for h in free if topo.die(h) == topo.die(c)][0]]
+        for u in range(2):
+            role[helpers[q][u]] = (q, u)
+    PLANS["p"] = (ring, partner, units, helpers, role)
+    return PLANS["p"]
+
+
 def rank_program(g, core, T, topo):
-    r = T.rank_of(core)
-    if r is None:
-        return
+    ring, partner, units, helpers, role = make_plan(T, topo)
     cores, S = T.cores, T.sem
-    sy, sc, pe, ve = g.sync, g.scalar, g.tensor, g.vector
-
-    def ring_of(q):
-        return sorted([q] + [k for k in range(N) if topo.same_plane(cores[q], cores[k])])
-
-    def order_of(q):
-        ring = ring_of(q)
-        s = ring.index(q)
-        return [ring[(s + i) % G] for i in range(1, G)] + [q]
-
-    def partner_of(q):
-        return [k for k in range(N) if topo.rack(topo.host(cores[k])) != topo.rack(topo.host(cores[q]))
-                and topo.chip(cores[k]) == topo.chip(cores[q]) and topo.may_write(cores[q], cores[k])][0]
+    add = AluOpType.add
 
     def engines(dst):
         m = topo.mask(core, dst)
@@ -62,130 +89,159 @@ def rank_program(g, core, T, topo):
     def bits(es):
         return sum(1 << e for e in es)
 
-    def runs_of(ks):
-        runs = []
-        for at, k in enumerate(ks):
-            if runs and runs[-1][1] + runs[-1][2] == k:
-                runs[-1][2] += 1
-            else:
-                runs.append([at, k, 1])
-        return runs
+    def transfer(dst_core, es, sem, src, dst):
+        rid, pid = topo.addr(dst_core, core)
+        return RemoteDMATransfer(dst_ids=[DstId(rid=rid, pnc=pid)], dma_engine_mask=bits(es), remote_sem=sem, src=src, dst=dst)
 
-    mine = order_of(r)
-    pr = partner_of(r)
-    theirs = order_of(pr)
-    ring = ring_of(r)
-    pos = ring.index(r)
+    def write(dst_core, es, sem, src, dst):
+        rid, pid = topo.addr(dst_core, core)
+        g.remote_dma(out_ap=dst, in_ap=src, remote_sem=sem, local_sem=S.sent, pid=pid, routing_id=rid,
+                     dma_engine_mask=bits(es))
+        return len(es)
 
-    near = sorted(mine)
-    sy.dma_start(blk(T.win, O_AT[0]), T.x[:]).then_inc(S.lx0, 16)
-    for at, k, n in runs_of(theirs[0:3]):
-        sc.dma_start(blk(T.dys, k, n), blk(T.dy, k, n)).then_inc(S.lda, 16)
+    if core in role:
+        q, u = role[core]
+        a, b = units[q][u]
+        at = ring[q].index(q)
+        twin = helpers[partner[q]][u]
+        n_in = len(engines(cores[q]))
+        ve = g.vector
+        ve.wait_ge(S.ho, n_in // 2)
+        ve.tensor_copy(blk(T.hb, 4), blk(T.hb, 0)).then_inc(S.ocp, 1)
+        ve.wait_ge(S.hst, n_in)
+        ve.wait_ge(S.hp, 8)
+        ve.tensor_tensor(blk(T.hb, 1), blk(T.hl, 0), blk(T.hs, 2), add).then_inc(S.sa, 1)
+        ve.tensor_tensor(blk(T.hb, 3), blk(T.hl, 1), blk(T.hs, 3), add).then_inc(S.sb, 1)
+        sent = 0
+        g.wait_ge(S.ho, n_in // 2)
+        sent += write(twin, engines(twin), S.hpx, blk(T.hb, 0), blk(T.hb, 2))
+        g.wait_ge(S.hst, n_in)
+        sent += write(twin, engines(twin), S.hp, blk(T.hs, 0, 2), blk(T.hl, 0, 2))
+        g.wait_ge(S.hpx, 8)
+        g.wait_ge(S.hp, 8)
+        g.wait_ge(S.ocp, 1)
+        g.wait_ge(S.sa, 1)
+        g.wait_ge(S.sb, 1)
+        ea, eb = engines(cores[a])[0:4], engines(cores[b])[4:8]
+        g.remote_dma_fused([transfer(cores[a], ea, S["w%d" % at], blk(T.hb, 0, 3), blk(T.rxw, 3 * at, 3)),
+                            transfer(cores[b], eb, S["w%d" % at], blk(T.hb, 2, 3), blk(T.rxw, 3 * at, 3))], local_sem=S.sent)
+        sent += 8
+        g.wait_ge(S.sent, sent)
+        return
+
+    r = T.rank_of(core)
+    if r is None:
+        return
+    sy, sc, pe, ve = g.sync, g.scalar, g.tensor, g.vector
+    pr = partner[r]
+    tm, tp = units[r], units[pr]
+    mate = tm[2][0]
+
+    def load(queue, ks, sem):
+        rs = runs_of(ks)
+        for k, n in rs:
+            queue.dma_start(blk(T.dys, k, n), blk(T.dy, k, n)).then_inc(sem, 16)
+        return 16 * len(rs)
+
+    sy.dma_start(blk(T.hb, 0), T.x[:]).then_inc(S.lx, 16)
+    n_f0 = load(sc, tp[0], S.lf0)
     sy.dma_start(T.wts[:], T.wt[:]).then_inc(S.lwt, 16)
-    for at, k, n in runs_of(theirs[3:6]):
-        sc.dma_start(blk(T.dys, k, n), blk(T.dy, k, n)).then_inc(S.ldb, 16)
-    sy.dma_start(blk(T.dys, near[0], G), blk(T.dy, near[0], G)).then_inc(S.ldm, 16)
-    sy.dma_start(T.dyts[:], T.dyt[:]).then_inc(S.ldt, 16)
+    n_n = load(sc, ring[r], S.ln)
+    n_f1 = load(sy, tp[1], S.lf1)
+    n_f2 = load(sc, tp[2], S.lf2)
+
+    landed = []
+    for u in range(2):
+        for q in ring[r]:
+            if q != r and r in units[q][u]:
+                at = ring[q].index(q)
+                first = units[q][u][0] == r
+                ends = [q, partner[q]] if first else [partner[q], q]
+                landed.append((S["w%d" % at], 4, blk(T.rxw, 3 * at + 1),
+                               [(blk(T.rxw, 3 * at), ends[0]), (blk(T.rxw, 3 * at + 2), ends[1])]))
+    landed.append((S.wm, 8, blk(T.rxm, 1), [(blk(T.rxm, 0), mate), (blk(T.rxm, 2), partner[mate])]))
 
     def partials(ks, bank, sem):
-        for at, k, n in runs_of(ks):
-            pe.matmul(blk(bank, at, n), T.wts[:], blk(T.dys, k, n), True, True).then_inc(sem, 1)
-        return len(runs_of(ks))
+        for i, k in enumerate(ks):
+            pe.matmul(blk(bank, i), T.wts[:], blk(T.dys, k), True, True).then_inc(sem, 1)
 
     pe.wait_ge(S.lwt, 16)
-    pe.wait_ge(S.lda, 16 * len(runs_of(theirs[0:3])))
-    n0 = partials(theirs[0:3], T.ps0, S.mm0)
-    pe.wait_ge(S.ldb, 16 * len(runs_of(theirs[3:6])))
-    n1 = partials(theirs[3:6], T.ps1, S.mm1)
-    pe.wait_ge(S.ldm, 16)
-    n2 = partials(mine[0:4], T.ps2, S.mm2)
-    n3 = partials(mine[4:6], T.ps3, S.mm3)
+    pe.wait_ge(S.lf0, n_f0)
+    pe.wait_ge(S.ln, n_n)
+    partials(tp[0] + tm[0], T.ps0, S.mm0)
+    pe.wait_ge(S.lf1, n_f1)
+    partials(tp[1] + tm[1], T.ps1, S.mm1)
+    pe.wait_ge(S.lf2, n_f2)
+    partials(tp[2], T.ps2, S.mm2)
+    partials(tm[2], T.ps3, S.mmr)
+    pe.wait_ge(S.idy, 1)
+    for j in range(N):
+        pe.matmul(blk(T["pt%d" % (j // 4)], j % 4), blk(T.dys, j), T.idn[:], True, True).then_inc(S["tp%d" % (j // 4)], 1)
     dwp = blk(T.psw, 0)
-    pe.wait_ge(S.lx0, 16)
-    pe.wait_ge(S.ldt, 16)
-    pe.matmul(dwp, blk(T.win, O_AT[0]), blk(T.dyts, r), True, False)
-    pe.wait_ge(S.xarr, 8)
-    pe.matmul(dwp, blk(T.win, P_AT[0]), blk(T.dyts, pr), False, False)
-    for i in range(1, G):
-        src = ring[(pos - i) % G]
-        o, p = WINDOW[i][1], WINDOW[i][2]
-        pe.wait_ge(S["arr%d" % i], ENGINES_OF[i])
-        pe.matmul(dwp, blk(T.rx, 3 * (i - 1) + o), blk(T.dyts, src), False, False)
-        if i < G - 1:
-            pe.matmul(dwp, blk(T.rx, 3 * (i - 1) + p), blk(T.dyts, partner_of(src)), False, False)
-        else:
-            pe.matmul(dwp, blk(T.rx, 3 * (i - 1) + p), blk(T.dyts, partner_of(src)), False, True).then_inc(S.mmw, 1)
+    pe.wait_ge(S.lx, 16)
+    for k in range(3):
+        pe.wait_ge(S["tc%d" % k], 1)
+    pe.matmul(dwp, blk(T.hb, 0), blk(T.dyts, r), True, False)
+    pe.wait_ge(S.hp, 8)
+    pe.matmul(dwp, blk(T.hb, 2), blk(T.dyts, pr), False, False)
+    for i, (sem, cnt, sb, xs) in enumerate(landed):
+        pe.wait_ge(sem, cnt)
+        for j, (xb, q) in enumerate(xs):
+            if i == len(landed) - 1 and j == len(xs) - 1:
+                pe.matmul(dwp, xb, blk(T.dyts, q), False, True).then_inc(S.mmw, 1)
+            else:
+                pe.matmul(dwp, xb, blk(T.dyts, q), False, False)
 
-    add = AluOpType.add
-    ve.wait_ge(S.lx0, 16)
-    ve.tensor_copy(blk(T.win, O_AT[1]), blk(T.win, O_AT[0])).then_inc(S.ocp, 1)
-    ve.tensor_copy(blk(T.win, O_AT[2]), blk(T.win, O_AT[0])).then_inc(S.ocp, 1)
-    ve.wait_ge(S.mm0, n0)
-    ve.tensor_copy(blk(T.pack, 0, 3), blk(T.ps0, 0, 3)).then_inc(S.cpa, 1)
-    ve.wait_ge(S.mm1, n1)
-    ve.tensor_copy(blk(T.pack, 3, 3), blk(T.ps1, 0, 3)).then_inc(S.cpb, 1)
-    ve.wait_ge(S.xarr, 8)
-    ve.tensor_copy(blk(T.win, P_AT[1]), blk(T.win, P_AT[0])).then_inc(S.pcp, 1)
-    ve.tensor_copy(blk(T.win, P_AT[2]), blk(T.win, P_AT[0])).then_inc(S.pcp, 1)
-    ve.wait_ge(S.mm2, n2)
-    ve.wait_ge(S.pa, 8)
-    ve.tensor_tensor(blk(T.win, 2), blk(T.ps2, 0), blk(T.land, 0), add).then_inc(S.s1, 1)
-    ve.tensor_tensor(blk(T.win, 3), blk(T.ps2, 1), blk(T.land, 1), add).then_inc(S.s2, 1)
-    ve.tensor_tensor(blk(T.win, 6), blk(T.ps2, 2), blk(T.land, 2), add).then_inc(S.s3, 1)
-    ve.wait_ge(S.pb, 8)
-    ve.tensor_tensor(blk(T.win, 7), blk(T.ps2, 3), blk(T.land, 3), add).then_inc(S.s4, 1)
-    ve.wait_ge(S.mm3, n3)
-    ve.tensor_tensor(blk(T.win, 10), blk(T.ps3, 0), blk(T.land, 4), add).then_inc(S.s5, 1)
+    for k in range(3):
+        sc.wait_ge(S["tp%d" % k], 4)
+        sc.activation(blk(T.dyts, 4 * k, 4), T["pt%d" % k][:], ActivationFunctionType.Copy).then_inc(S["tc%d" % k], 1)
+
+    ve.memset(T.ones[:], 1.0).then_inc(S.one, 1)
+    ve.wait_ge(S.lx, 16)
+    ve.tensor_copy(blk(T.pack, 1), blk(T.hb, 0)).then_inc(S.xcp, 1)
+    ve.wait_ge(S.mm0, 4)
+    ve.tensor_copy(blk(T.stg, 0, 4), blk(T.ps0, 0, 4)).then_inc(S.cs0, 1)
+    ve.wait_ge(S.mm1, 4)
+    ve.tensor_copy(blk(T.stg, 4, 4), blk(T.ps1, 0, 4)).then_inc(S.cs1, 1)
+    ve.wait_ge(S.mm2, 2)
+    ve.tensor_copy(blk(T.pack, 0), blk(T.ps2, 0)).then_inc(S.cp2, 1)
+    ve.tensor_copy(blk(T.pack, 2), blk(T.ps2, 1)).then_inc(S.cp2, 1)
+    ve.wait_ge(S.mmr, 2)
+    ve.wait_ge(S.hp, 8)
+    ve.tensor_tensor(blk(T.hb, 1), blk(T.ps3, 0), blk(T.hb, 1), add).then_inc(S.s5, 1)
     acc = blk(T.ps3, 1)
-    ve.tensor_tensor(acc, acc, blk(T.land, 5), add).then_inc(S.acc, 1)
-    for i in range(1, G):
-        ve.wait_ge(S["arr%d" % i], ENGINES_OF[i])
-        ve.wait_ge(S.acc, i)
-        out = acc if i < G - 1 else T.dxs[:]
-        ve.tensor_tensor(out, acc, blk(T.rx, 3 * (i - 1) + WINDOW[i][3]), add).then_inc(S.acc, 1)
+    ve.tensor_tensor(acc, acc, blk(T.hb, 3), add).then_inc(S.acc, 1)
+    for i, (sem, cnt, sb, xs) in enumerate(landed):
+        ve.wait_ge(sem, cnt)
+        ve.wait_ge(S.acc, i + 1)
+        out = acc if i < len(landed) - 1 else T.dxs[:]
+        ve.tensor_tensor(out, acc, sb, add).then_inc(S.acc, 1)
     ve.wait_ge(S.mmw, 1)
     ve.tensor_copy(T.dws[:], dwp).then_inc(S.dwc, 1)
 
-    sy.wait_ge(S.acc, G)
+    sy.wait_ge(S.acc, len(landed) + 1)
     sy.dma_start(T.dx[:], T.dxs[:]).then_inc(S.stx, 16)
     sc.wait_ge(S.dwc, 1)
     sc.dma_start(T.dw[:], T.dws[:]).then_inc(S.stw, 16)
 
-    pc = cores[pr]
-    rid, pid = topo.addr(pc, core)
-    cable = bits(engines(pc))
-    g.wait_ge(S.lx0, 16)
-    g.remote_dma(out_ap=blk(T.win, P_AT[0]), in_ap=blk(T.win, O_AT[0]), remote_sem=S.xarr, local_sem=S.sent,
-                 pid=pid, routing_id=rid, dma_engine_mask=cable)
-    g.wait_ge(S.cpa, 1)
-    g.remote_dma(out_ap=blk(T.land, 0, 3), in_ap=blk(T.pack, 0, 3), remote_sem=S.pa, local_sem=S.sent,
-                 pid=pid, routing_id=rid, dma_engine_mask=cable)
-    g.wait_ge(S.cpb, 1)
-    g.remote_dma(out_ap=blk(T.land, 3, 3), in_ap=blk(T.pack, 3, 3), remote_sem=S.pb, local_sem=S.sent,
-                 pid=pid, routing_id=rid, dma_engine_mask=cable)
-    sent = 24
-    needs = {1: ("s1",), 2: ("s2", "pcp", "ocp"), 3: ("s3", "pcp", "ocp"), 4: ("s4", "pcp", "ocp"), 5: ("s5", "pcp", "ocp")}
-    full = {"s1": 1, "s2": 1, "s3": 1, "s4": 1, "s5": 1, "pcp": 2, "ocp": 2}
-    g.wait_ge(S.xarr, 8)
-    waited = []
-    for call in PLAN:
-        for s, n in call:
-            for name in needs[s]:
-                if name not in waited:
-                    waited.append(name)
-                    g.wait_ge(S[name], full[name])
-        used = 0
-        trs = []
-        for s, n in call:
-            d = cores[mine[s - 1]]
-            es = engines(d)[used:used + n]
-            used += n
-            drid, dpid = topo.addr(d, core)
-            trs.append(RemoteDMATransfer(dst_ids=[DstId(rid=drid, pnc=dpid)], dma_engine_mask=bits(es),
-                                         remote_sem=S["arr%d" % s], src=blk(T.win, WINDOW[s][0], 3),
-                                         dst=blk(T.rx, 3 * (s - 1), 3)))
-            sent += n
-        g.remote_dma_fused(trs, local_sem=S.sent)
+    h0, h1 = helpers[r]
+    inside = engines(h0)
+    half = len(inside) // 2
+    g.wait_ge(S.one, 1)
+    g.affine_select(T.idn[:], T.ones[:], [[-1, B]], AluOpType.is_equal, 0.0, 0, 1).then_inc(S.idy, 1)
+    g.wait_ge(S.lx, 16)
+    g.remote_dma_fused([transfer(h0, inside[:half], S.ho, blk(T.hb, 0), blk(T.hb, 0)),
+                        transfer(h1, inside[half:], S.ho, blk(T.hb, 0), blk(T.hb, 0))], local_sem=S.sent)
+    sent = len(inside)
+    for u in range(2):
+        g.wait_ge(S["cs%d" % u], 1)
+        sent += write(helpers[r][u], inside, S.hst, blk(T.stg, 4 * u, 4), blk(T.hs, 0, 4))
+    g.wait_ge(S.xcp, 1)
+    g.wait_ge(S.cp2, 2)
+    sent += write(cores[pr], engines(cores[pr]), S.hp, blk(T.pack, 0, 3), blk(T.hb, 1, 3))
+    g.wait_ge(S.hp, 8)
+    g.wait_ge(S.s5, 1)
+    sent += write(cores[mate], engines(cores[mate]), S.wm, blk(T.hb, 0, 3), blk(T.rxm, 0, 3))
     g.wait_ge(S.sent, sent)
     g.wait_ge(S.stx, 16)
     g.wait_ge(S.stw, 16)

@@ -7,16 +7,17 @@ G = 6
 WORLD = 512
 
 SCRATCH = {
-    "hb": ("sbuf", [128, 5 * B], "bfloat16"),
-    "hs": ("sbuf", [128, 4 * B], "bfloat16"),
-    "hl": ("sbuf", [128, 2 * B], "bfloat16"),
+    "hb": ("sbuf", [128, 2 * B], "bfloat16"),
+    "xs": ("sbuf", [128, B], "bfloat16"),
     "wts": ("sbuf", [128, B], "bfloat16"),
     "dys": ("sbuf", [128, N * B], "bfloat16"),
     "dyts": ("sbuf", [128, N * B], "bfloat16"),
-    "stg": ("sbuf", [128, 8 * B], "bfloat16"),
-    "pack": ("sbuf", [128, 3 * B], "bfloat16"),
-    "rxw": ("sbuf", [128, 3 * G * B], "bfloat16"),
-    "rxm": ("sbuf", [128, 3 * B], "bfloat16"),
+    "stg": ("sbuf", [128, 10 * B], "bfloat16"),
+    "rxp": ("sbuf", [128, 2 * G * B], "bfloat16"),
+    "rxx": ("sbuf", [128, 2 * G * B], "bfloat16"),
+    "px": ("sbuf", [128, B], "bfloat16"),
+    "sp": ("sbuf", [128, B], "bfloat16"),
+    "rs": ("sbuf", [128, B], "bfloat16"),
     "ones": ("sbuf", [128, B], "bfloat16"),
     "idn": ("sbuf", [128, B], "bfloat16"),
     "dxs": ("sbuf", [128, B], "bfloat16"),
@@ -30,10 +31,12 @@ SCRATCH = {
     "pt1": ("psum", [128, 512], "float32"),
     "pt2": ("psum", [128, 512], "float32"),
 }
-SEMAPHORES = ["lx", "lwt", "lf0", "lf1", "lf2", "ln", "one", "idy",
+SEMAPHORES = ["lx", "lwt", "lf0", "lf1", "lf2", "one", "idy",
               "mm0", "mm1", "mm2", "mmr", "mmw", "tp0", "tp1", "tp2", "tc0", "tc1", "tc2",
-              "xcp", "cs0", "cs1", "cp2", "s5", "ocp", "sa", "sb", "acc", "dwc",
-              "ho", "hst", "hpx", "hp", "w0", "w1", "w2", "w3", "w4", "w5", "wm", "sent", "stx", "stw"]
+              "cs0", "cs1", "cs2", "acc", "sps", "dxc", "dwc",
+              "ho", "hpx", "hp", "ss",
+              "pw0", "pw1", "pw2", "pw3", "pw4", "pw5", "xw0", "xw1", "xw2", "xw3", "xw4", "xw5",
+              "sent", "stx", "stw"]
 
 PLANS = {}
 
@@ -56,29 +59,24 @@ def make_plan(T, topo):
     if "p" in PLANS:
         return PLANS["p"]
     cores = list(T.cores)
-    ring, partner, units, helpers, role = {}, {}, {}, {}, {}
+    ring, partner, helpers, role = {}, {}, {}, {}
     for q in range(N):
         ring[q] = sorted([q] + [k for k in range(N) if topo.same_plane(cores[q], cores[k])])
         partner[q] = [k for k in range(N) if topo.rack(topo.host(cores[k])) != topo.rack(topo.host(cores[q]))
                       and topo.chip(cores[k]) == topo.chip(cores[q]) and topo.may_write(cores[q], cores[k])][0]
     for q in range(N):
-        rg = ring[q]
-        gq = rg.index(q) // 2
-        pairs = [[rg[2 * i], rg[2 * i + 1]] for i in range(G // 2)]
-        mate = [k for k in pairs[gq] if k != q][0]
-        units[q] = [pairs[(gq + 1) % 3], pairs[(gq + 2) % 3], [mate, q]]
         c = cores[q]
         free = [h for h in range(WORLD) if h not in cores and topo.host(h) == topo.host(c) and topo.chip(h) == topo.chip(c)
-                and all(topo.may_write(h, cores[k]) for k in rg if k != q)]
-        helpers[q] = [[h for h in free if topo.die(h) != topo.die(c)][0], [h for h in free if topo.die(h) == topo.die(c)][0]]
+                and all(topo.may_write(h, cores[k]) for k in ring[q] if k != q)]
+        helpers[q] = [h for h in free if topo.die(h) != topo.die(c)][0:2]
         for u in range(2):
             role[helpers[q][u]] = (q, u)
-    PLANS["p"] = (ring, partner, units, helpers, role)
+    PLANS["p"] = (ring, partner, helpers, role)
     return PLANS["p"]
 
 
 def rank_program(g, core, T, topo):
-    ring, partner, units, helpers, role = make_plan(T, topo)
+    ring, partner, helpers, role = make_plan(T, topo)
     cores, S = T.cores, T.sem
     add = AluOpType.add
 
@@ -99,33 +97,29 @@ def rank_program(g, core, T, topo):
                      dma_engine_mask=bits(es))
         return len(es)
 
+    def two(ka, kb, sem, src_a, src_b, dst):
+        es = engines(cores[ka])
+        h = len(es) // 2
+        g.remote_dma_fused([transfer(cores[ka], es[:h], sem, src_a, dst),
+                            transfer(cores[kb], es[h:], sem, src_b, dst)], local_sem=S.sent)
+        return len(es)
+
     if core in role:
         q, u = role[core]
-        a, b = units[q][u]
-        at = ring[q].index(q)
-        twin = helpers[partner[q]][u]
-        n_in = len(engines(cores[q]))
-        ve = g.vector
-        ve.wait_ge(S.ho, n_in // 2)
-        ve.tensor_copy(blk(T.hb, 4), blk(T.hb, 0)).then_inc(S.ocp, 1)
-        ve.wait_ge(S.hst, n_in)
-        ve.wait_ge(S.hp, 8)
-        ve.tensor_tensor(blk(T.hb, 1), blk(T.hl, 0), blk(T.hs, 2), add).then_inc(S.sa, 1)
-        ve.tensor_tensor(blk(T.hb, 3), blk(T.hl, 1), blk(T.hs, 3), add).then_inc(S.sb, 1)
-        sent = 0
-        g.wait_ge(S.ho, n_in // 2)
-        sent += write(twin, engines(twin), S.hpx, blk(T.hb, 0), blk(T.hb, 2))
-        g.wait_ge(S.hst, n_in)
-        sent += write(twin, engines(twin), S.hp, blk(T.hs, 0, 2), blk(T.hl, 0, 2))
-        g.wait_ge(S.hpx, 8)
-        g.wait_ge(S.hp, 8)
-        g.wait_ge(S.ocp, 1)
-        g.wait_ge(S.sa, 1)
-        g.wait_ge(S.sb, 1)
-        ea, eb = engines(cores[a])[0:4], engines(cores[b])[4:8]
-        g.remote_dma_fused([transfer(cores[a], ea, S["w%d" % at], blk(T.hb, 0, 3), blk(T.rxw, 3 * at, 3)),
-                            transfer(cores[b], eb, S["w%d" % at], blk(T.hb, 2, 3), blk(T.rxw, 3 * at, 3))], local_sem=S.sent)
-        sent += 8
+        rg = ring[q]
+        at = rg.index(q)
+        after = [rg[(at + d) % G] for d in range(G)]
+        out = engines(cores[after[1]])
+        quarter = (len(engines(cores[q])) - len(out)) // 2
+        win, dst, sem = blk(T.hb, 0, 2), blk(T.rxx, 2 * at, 2), S["xw%d" % at]
+        g.wait_ge(S.ho, quarter)
+        g.wait_ge(S.hpx, len(out) // 2)
+        if u == 0:
+            sent = two(after[1], after[2], sem, win, win, dst)
+            sent += write(cores[after[3]], out, sem, win, dst)
+        else:
+            sent = two(after[4], after[5], sem, win, win, dst)
+            sent += write(cores[q], out, S.hp, blk(T.hb, 1), T.px[:])
         g.wait_ge(S.sent, sent)
         return
 
@@ -134,8 +128,15 @@ def rank_program(g, core, T, topo):
         return
     sy, sc, pe, ve = g.sync, g.scalar, g.tensor, g.vector
     pr = partner[r]
-    tm, tp = units[r], units[pr]
-    mate = tm[2][0]
+    rg = ring[r]
+    at = rg.index(r)
+    after = [rg[(at + d) % G] for d in range(G)]
+    before = [(at - d) % G for d in range(G)]
+    out = engines(cores[pr])
+    full, half = len(out), len(out) // 2
+    order = []
+    for k in after[1:]:
+        order += [partner[k], k]
 
     def load(queue, ks, sem):
         rs = runs_of(ks)
@@ -143,23 +144,11 @@ def rank_program(g, core, T, topo):
             queue.dma_start(blk(T.dys, k, n), blk(T.dy, k, n)).then_inc(sem, 16)
         return 16 * len(rs)
 
-    sy.dma_start(blk(T.hb, 0), T.x[:]).then_inc(S.lx, 16)
-    n_f0 = load(sc, tp[0], S.lf0)
+    sy.dma_start(T.xs[:], T.x[:]).then_inc(S.lx, 16)
+    n_f0 = load(sc, order[0:4], S.lf0)
     sy.dma_start(T.wts[:], T.wt[:]).then_inc(S.lwt, 16)
-    n_n = load(sc, ring[r], S.ln)
-    n_f1 = load(sy, tp[1], S.lf1)
-    n_f2 = load(sc, tp[2], S.lf2)
-
-    landed = []
-    for u in range(2):
-        for q in ring[r]:
-            if q != r and r in units[q][u]:
-                at = ring[q].index(q)
-                first = units[q][u][0] == r
-                ends = [q, partner[q]] if first else [partner[q], q]
-                landed.append((S["w%d" % at], 4, blk(T.rxw, 3 * at + 1),
-                               [(blk(T.rxw, 3 * at), ends[0]), (blk(T.rxw, 3 * at + 2), ends[1])]))
-    landed.append((S.wm, 8, blk(T.rxm, 1), [(blk(T.rxm, 0), mate), (blk(T.rxm, 2), partner[mate])]))
+    n_f1 = load(sy, order[4:8], S.lf1)
+    n_f2 = load(sc, order[8:10] + [pr, r], S.lf2)
 
     def partials(ks, bank, sem):
         for i, k in enumerate(ks):
@@ -167,13 +156,12 @@ def rank_program(g, core, T, topo):
 
     pe.wait_ge(S.lwt, 16)
     pe.wait_ge(S.lf0, n_f0)
-    pe.wait_ge(S.ln, n_n)
-    partials(tp[0] + tm[0], T.ps0, S.mm0)
+    partials(order[0:4], T.ps0, S.mm0)
     pe.wait_ge(S.lf1, n_f1)
-    partials(tp[1] + tm[1], T.ps1, S.mm1)
+    partials(order[4:8], T.ps1, S.mm1)
     pe.wait_ge(S.lf2, n_f2)
-    partials(tp[2], T.ps2, S.mm2)
-    partials(tm[2], T.ps3, S.mmr)
+    partials(order[8:10], T.ps2, S.mm2)
+    partials([pr, r], T.ps3, S.mmr)
     pe.wait_ge(S.idy, 1)
     for j in range(N):
         pe.matmul(blk(T["pt%d" % (j // 4)], j % 4), blk(T.dys, j), T.idn[:], True, True).then_inc(S["tp%d" % (j // 4)], 1)
@@ -181,67 +169,71 @@ def rank_program(g, core, T, topo):
     pe.wait_ge(S.lx, 16)
     for k in range(3):
         pe.wait_ge(S["tc%d" % k], 1)
-    pe.matmul(dwp, blk(T.hb, 0), blk(T.dyts, r), True, False)
-    pe.wait_ge(S.hp, 8)
-    pe.matmul(dwp, blk(T.hb, 2), blk(T.dyts, pr), False, False)
-    for i, (sem, cnt, sb, xs) in enumerate(landed):
-        pe.wait_ge(sem, cnt)
-        for j, (xb, q) in enumerate(xs):
-            if i == len(landed) - 1 and j == len(xs) - 1:
-                pe.matmul(dwp, xb, blk(T.dyts, q), False, True).then_inc(S.mmw, 1)
-            else:
-                pe.matmul(dwp, xb, blk(T.dyts, q), False, False)
+    pe.matmul(dwp, T.xs[:], blk(T.dyts, r), True, False)
+    for d in (1, 2, 4, 5):
+        pe.wait_ge(S["xw%d" % before[d]], half)
+        pe.matmul(dwp, blk(T.rxx, 2 * before[d]), blk(T.dyts, rg[before[d]]), False, False)
+        pe.matmul(dwp, blk(T.rxx, 2 * before[d] + 1), blk(T.dyts, partner[rg[before[d]]]), False, False)
+    pe.wait_ge(S.hp, full)
+    pe.matmul(dwp, T.px[:], blk(T.dyts, pr), False, False)
+    pe.wait_ge(S["xw%d" % before[3]], full)
+    pe.matmul(dwp, blk(T.rxx, 2 * before[3]), blk(T.dyts, rg[before[3]]), False, False)
+    pe.matmul(dwp, blk(T.rxx, 2 * before[3] + 1), blk(T.dyts, partner[rg[before[3]]]), False, True).then_inc(S.mmw, 1)
 
+    copy = ActivationFunctionType.Copy
+    sc.wait_ge(S.mm1, 4)
+    sc.activation(blk(T.stg, 4, 4), T.ps1[:], copy).then_inc(S.cs1, 1)
     for k in range(3):
         sc.wait_ge(S["tp%d" % k], 4)
-        sc.activation(blk(T.dyts, 4 * k, 4), T["pt%d" % k][:], ActivationFunctionType.Copy).then_inc(S["tc%d" % k], 1)
-
-    ve.memset(T.ones[:], 1.0).then_inc(S.one, 1)
-    ve.wait_ge(S.lx, 16)
-    ve.tensor_copy(blk(T.pack, 1), blk(T.hb, 0)).then_inc(S.xcp, 1)
-    ve.wait_ge(S.mm0, 4)
-    ve.tensor_copy(blk(T.stg, 0, 4), blk(T.ps0, 0, 4)).then_inc(S.cs0, 1)
-    ve.wait_ge(S.mm1, 4)
-    ve.tensor_copy(blk(T.stg, 4, 4), blk(T.ps1, 0, 4)).then_inc(S.cs1, 1)
-    ve.wait_ge(S.mm2, 2)
-    ve.tensor_copy(blk(T.pack, 0), blk(T.ps2, 0)).then_inc(S.cp2, 1)
-    ve.tensor_copy(blk(T.pack, 2), blk(T.ps2, 1)).then_inc(S.cp2, 1)
-    ve.wait_ge(S.mmr, 2)
-    ve.wait_ge(S.hp, 8)
-    ve.tensor_tensor(blk(T.hb, 1), blk(T.ps3, 0), blk(T.hb, 1), add).then_inc(S.s5, 1)
-    acc = blk(T.ps3, 1)
-    ve.tensor_tensor(acc, acc, blk(T.hb, 3), add).then_inc(S.acc, 1)
-    for i, (sem, cnt, sb, xs) in enumerate(landed):
-        ve.wait_ge(sem, cnt)
-        ve.wait_ge(S.acc, i + 1)
-        out = acc if i < len(landed) - 1 else T.dxs[:]
-        ve.tensor_tensor(out, acc, sb, add).then_inc(S.acc, 1)
-    ve.wait_ge(S.mmw, 1)
-    ve.tensor_copy(T.dws[:], dwp).then_inc(S.dwc, 1)
-
-    sy.wait_ge(S.acc, len(landed) + 1)
-    sy.dma_start(T.dx[:], T.dxs[:]).then_inc(S.stx, 16)
+        sc.activation(blk(T.dyts, 4 * k, 4), T["pt%d" % k][:], copy).then_inc(S["tc%d" % k], 1)
+    sc.wait_ge(S.mmw, 1)
+    sc.activation(T.dws[:], dwp, copy).then_inc(S.dwc, 1)
     sc.wait_ge(S.dwc, 1)
     sc.dma_start(T.dw[:], T.dws[:]).then_inc(S.stw, 16)
 
+    ve.memset(T.ones[:], 1.0).then_inc(S.one, 1)
+    ve.wait_ge(S.mm0, 4)
+    ve.tensor_copy(blk(T.stg, 0, 4), blk(T.ps0, 0, 4)).then_inc(S.cs0, 1)
+    ve.wait_ge(S.mm2, 2)
+    ve.tensor_copy(blk(T.stg, 8, 2), blk(T.ps2, 0, 2)).then_inc(S.cs2, 1)
+    ve.wait_ge(S.mmr, 2)
+    both = blk(T.ps3, 0, 2)
+    for i, d in enumerate((1, 2, 3, 4)):
+        ve.wait_ge(S["pw%d" % before[d]], half)
+        if i:
+            ve.wait_ge(S.acc, i)
+        ve.tensor_tensor(both, both, blk(T.rxp, 2 * before[d], 2), add).then_inc(S.acc, 1)
+    ve.wait_ge(S["pw%d" % before[5]], full)
+    ve.wait_ge(S.acc, 4)
+    ve.tensor_tensor(T.sp[:], blk(T.ps3, 0), blk(T.rxp, 2 * before[5]), add).then_inc(S.sps, 1)
+    ve.tensor_tensor(blk(T.ps3, 1), blk(T.ps3, 1), blk(T.rxp, 2 * before[5] + 1), add).then_inc(S.acc, 1)
+    ve.wait_ge(S.ss, full)
+    ve.wait_ge(S.acc, 5)
+    ve.tensor_tensor(T.dxs[:], blk(T.ps3, 1), T.rs[:], add).then_inc(S.dxc, 1)
+
+    sy.wait_ge(S.dxc, 1)
+    sy.dma_start(T.dx[:], T.dxs[:]).then_inc(S.stx, 16)
+
     h0, h1 = helpers[r]
-    inside = engines(h0)
-    half = len(inside) // 2
+    f0, f1 = helpers[pr]
+    stay = [e for e in engines(h0) if e not in out]
     g.wait_ge(S.one, 1)
     g.affine_select(T.idn[:], T.ones[:], [[-1, B]], AluOpType.is_equal, 0.0, 0, 1).then_inc(S.idy, 1)
     g.wait_ge(S.lx, 16)
-    g.remote_dma_fused([transfer(h0, inside[:half], S.ho, blk(T.hb, 0), blk(T.hb, 0)),
-                        transfer(h1, inside[half:], S.ho, blk(T.hb, 0), blk(T.hb, 0))], local_sem=S.sent)
-    sent = len(inside)
-    for u in range(2):
-        g.wait_ge(S["cs%d" % u], 1)
-        sent += write(helpers[r][u], inside, S.hst, blk(T.stg, 4 * u, 4), blk(T.hs, 0, 4))
-    g.wait_ge(S.xcp, 1)
-    g.wait_ge(S.cp2, 2)
-    sent += write(cores[pr], engines(cores[pr]), S.hp, blk(T.pack, 0, 3), blk(T.hb, 1, 3))
-    g.wait_ge(S.hp, 8)
-    g.wait_ge(S.s5, 1)
-    sent += write(cores[mate], engines(cores[mate]), S.wm, blk(T.hb, 0, 3), blk(T.rxm, 0, 3))
+    g.remote_dma_fused([transfer(f0, out[:half], S.hpx, T.xs[:], blk(T.hb, 1)),
+                        transfer(f1, out[half:], S.hpx, T.xs[:], blk(T.hb, 1)),
+                        transfer(h0, stay[:len(stay) // 2], S.ho, T.xs[:], blk(T.hb, 0)),
+                        transfer(h1, stay[len(stay) // 2:], S.ho, T.xs[:], blk(T.hb, 0))], local_sem=S.sent)
+    sent = len(out) + len(stay)
+    mine, sem = blk(T.rxp, 2 * at, 2), S["pw%d" % at]
+    g.wait_ge(S.cs0, 1)
+    sent += two(after[1], after[2], sem, blk(T.stg, 0, 2), blk(T.stg, 2, 2), mine)
+    g.wait_ge(S.cs1, 1)
+    sent += two(after[3], after[4], sem, blk(T.stg, 4, 2), blk(T.stg, 6, 2), mine)
+    g.wait_ge(S.cs2, 1)
+    sent += write(cores[after[5]], out, sem, blk(T.stg, 8, 2), mine)
+    g.wait_ge(S.sps, 1)
+    sent += write(cores[pr], out, S.ss, T.sp[:], T.rs[:])
     g.wait_ge(S.sent, sent)
     g.wait_ge(S.stx, 16)
     g.wait_ge(S.stw, 16)

@@ -8,6 +8,7 @@ WORLD = 512
 
 SCRATCH = {
     "hb": ("sbuf", [128, 2 * B], "bfloat16"),
+    "bb": ("sbuf", [128, 4 * B], "bfloat16"),
     "xs": ("sbuf", [128, B], "bfloat16"),
     "wts": ("sbuf", [128, B], "bfloat16"),
     "dys": ("sbuf", [128, N * B], "bfloat16"),
@@ -34,8 +35,9 @@ SCRATCH = {
 SEMAPHORES = ["lx", "lwt", "lf0", "lf1", "lf2", "one", "idy",
               "mm0", "mm1", "mm2", "mmr", "mmw", "tp0", "tp1", "tp2", "tc0", "tc1", "tc2",
               "cs0", "cs1", "cs2", "acc", "sps", "dxc", "dwc",
-              "ho", "hpx", "hp", "ss",
-              "pw0", "pw1", "pw2", "pw3", "pw4", "pw5", "xw0", "xw1", "xw2", "xw3", "xw4", "xw5",
+              "ho", "hpx", "hp", "hbb", "ss", "xo",
+              "pa0", "pa1", "pa2", "pa3", "pa4", "pa5", "pb0", "pb1", "pb2", "pb3", "pb4", "pb5",
+              "xw0", "xw1", "xw2", "xw3", "xw4", "xw5",
               "sent", "stx", "stw"]
 
 PLANS = {}
@@ -68,8 +70,9 @@ def make_plan(T, topo):
         c = cores[q]
         free = [h for h in range(WORLD) if h not in cores and topo.host(h) == topo.host(c) and topo.chip(h) == topo.chip(c)
                 and all(topo.may_write(h, cores[k]) for k in ring[q] if k != q)]
-        helpers[q] = [h for h in free if topo.die(h) != topo.die(c)][0:2]
-        for u in range(2):
+        helpers[q] = ([h for h in free if topo.die(h) != topo.die(c)][0:2]
+                      + [h for h in free if topo.die(h) == topo.die(c)][0:1])
+        for u in range(3):
             role[helpers[q][u]] = (q, u)
     PLANS["p"] = (ring, partner, helpers, role)
     return PLANS["p"]
@@ -97,12 +100,14 @@ def rank_program(g, core, T, topo):
                      dma_engine_mask=bits(es))
         return len(es)
 
-    def two(ka, kb, sem, src_a, src_b, dst):
-        es = engines(cores[ka])
-        h = len(es) // 2
-        g.remote_dma_fused([transfer(cores[ka], es[:h], sem, src_a, dst),
-                            transfer(cores[kb], es[h:], sem, src_b, dst)], local_sem=S.sent)
-        return len(es)
+    def shares(ks, sem, srcs, dst):
+        es = engines(cores[ks[0]])
+        w = len(es) // len(ks)
+        return [transfer(cores[k], es[i * w:(i + 1) * w], sem, srcs[i], dst) for i, k in enumerate(ks)]
+
+    def spread(ks, sem, srcs, dst):
+        g.remote_dma_fused(shares(ks, sem, srcs, dst), local_sem=S.sent)
+        return len(engines(cores[ks[0]]))
 
     if core in role:
         q, u = role[core]
@@ -110,16 +115,25 @@ def rank_program(g, core, T, topo):
         at = rg.index(q)
         after = [rg[(at + d) % G] for d in range(G)]
         out = engines(cores[after[1]])
-        quarter = (len(engines(cores[q])) - len(out)) // 2
-        win, dst, sem = blk(T.hb, 0, 2), blk(T.rxx, 2 * at, 2), S["xw%d" % at]
-        g.wait_ge(S.ho, quarter)
-        g.wait_ge(S.hpx, len(out) // 2)
+        stay = [e for e in engines(cores[q]) if e not in out]
+        o, p = blk(T.hb, 0), blk(T.hb, 1)
+        dst_o, dst_p, sem = blk(T.rxx, 2 * at), blk(T.rxx, 2 * at + 1), S["xw%d" % at]
+        g.wait_ge(S.ho, len(stay) // 2 if u == 0 else len(stay) // 4)
         if u == 0:
-            sent = two(after[1], after[2], sem, win, win, dst)
-            sent += write(cores[after[3]], out, sem, win, dst)
+            sent = write(cores[after[1]], out, S.xo, o, dst_o)
+            g.wait_ge(S.hpx, len(out))
+            inner = stay[:len(stay) // 2]
+            g.remote_dma_fused(shares(after[1:5], sem, [p] * 4, dst_p)
+                               + [transfer(cores[q], inner, S.hp, p, T.px[:])], local_sem=S.sent)
+            sent += len(out) + len(inner)
+            sent += write(cores[after[5]], out, sem, p, dst_p)
+        elif u == 1:
+            sent = spread(after[4:6], S.xo, [o, o], dst_o)
+            sent += write(cores[after[2]], out, S.xo, o, dst_o)
         else:
-            sent = two(after[4], after[5], sem, win, win, dst)
-            sent += write(cores[q], out, S.hp, blk(T.hb, 1), T.px[:])
+            sent = write(cores[after[3]], out, S.xo, o, dst_o)
+            g.wait_ge(S.hbb, len(stay))
+            sent += spread(after[1:5], S["pb%d" % at], [blk(T.bb, i) for i in range(4)], blk(T.rxp, 2 * at + 1))
         g.wait_ge(S.sent, sent)
         return
 
@@ -133,10 +147,9 @@ def rank_program(g, core, T, topo):
     after = [rg[(at + d) % G] for d in range(G)]
     before = [(at - d) % G for d in range(G)]
     out = engines(cores[pr])
-    full, half = len(out), len(out) // 2
-    order = []
-    for k in after[1:]:
-        order += [partner[k], k]
+    full, half, quarter = len(out), len(out) // 2, len(out) // 4
+    order = ([partner[k] for k in after[1:5]] + after[1:5]
+             + [partner[after[5]], after[5]])
 
     def load(queue, ks, sem):
         rs = runs_of(ks)
@@ -170,15 +183,16 @@ def rank_program(g, core, T, topo):
     for k in range(3):
         pe.wait_ge(S["tc%d" % k], 1)
     pe.matmul(dwp, T.xs[:], blk(T.dyts, r), True, False)
-    for d in (1, 2, 4, 5):
-        pe.wait_ge(S["xw%d" % before[d]], half)
+    pe.wait_ge(S.xo, 3 * full + 2 * half)
+    for d in range(1, G):
         pe.matmul(dwp, blk(T.rxx, 2 * before[d]), blk(T.dyts, rg[before[d]]), False, False)
-        pe.matmul(dwp, blk(T.rxx, 2 * before[d] + 1), blk(T.dyts, partner[rg[before[d]]]), False, False)
-    pe.wait_ge(S.hp, full)
+    pe.wait_ge(S.hp, half)
     pe.matmul(dwp, T.px[:], blk(T.dyts, pr), False, False)
-    pe.wait_ge(S["xw%d" % before[3]], full)
-    pe.matmul(dwp, blk(T.rxx, 2 * before[3]), blk(T.dyts, rg[before[3]]), False, False)
-    pe.matmul(dwp, blk(T.rxx, 2 * before[3] + 1), blk(T.dyts, partner[rg[before[3]]]), False, True).then_inc(S.mmw, 1)
+    for d in (1, 2, 3, 4):
+        pe.wait_ge(S["xw%d" % before[d]], quarter)
+        pe.matmul(dwp, blk(T.rxx, 2 * before[d] + 1), blk(T.dyts, partner[rg[before[d]]]), False, False)
+    pe.wait_ge(S["xw%d" % before[5]], full)
+    pe.matmul(dwp, blk(T.rxx, 2 * before[5] + 1), blk(T.dyts, partner[rg[before[5]]]), False, True).then_inc(S.mmw, 1)
 
     copy = ActivationFunctionType.Copy
     sc.wait_ge(S.mm1, 4)
@@ -197,41 +211,50 @@ def rank_program(g, core, T, topo):
     ve.wait_ge(S.mm2, 2)
     ve.tensor_copy(blk(T.stg, 8, 2), blk(T.ps2, 0, 2)).then_inc(S.cs2, 1)
     ve.wait_ge(S.mmr, 2)
-    both = blk(T.ps3, 0, 2)
-    for i, d in enumerate((1, 2, 3, 4)):
-        ve.wait_ge(S["pw%d" % before[d]], half)
-        if i:
-            ve.wait_ge(S.acc, i)
-        ve.tensor_tensor(both, both, blk(T.rxp, 2 * before[d], 2), add).then_inc(S.acc, 1)
-    ve.wait_ge(S["pw%d" % before[5]], full)
-    ve.wait_ge(S.acc, 4)
-    ve.tensor_tensor(T.sp[:], blk(T.ps3, 0), blk(T.rxp, 2 * before[5]), add).then_inc(S.sps, 1)
-    ve.tensor_tensor(blk(T.ps3, 1), blk(T.ps3, 1), blk(T.rxp, 2 * before[5] + 1), add).then_inc(S.acc, 1)
+    for_p, for_me = blk(T.ps3, 0), blk(T.ps3, 1)
+    n_acc = 0
+    for d in (1, 2, 3, 4):
+        ve.wait_ge(S["pa%d" % before[d]], quarter)
+        if n_acc:
+            ve.wait_ge(S.acc, n_acc)
+        ve.tensor_tensor(for_p, for_p, blk(T.rxp, 2 * before[d]), add).then_inc(S.acc, 1)
+        n_acc += 1
+    ve.wait_ge(S["pa%d" % before[5]], full)
+    ve.wait_ge(S.acc, n_acc)
+    ve.tensor_tensor(T.sp[:], for_p, blk(T.rxp, 2 * before[5]), add).then_inc(S.sps, 1)
+    ve.tensor_tensor(for_me, for_me, blk(T.rxp, 2 * before[5] + 1), add).then_inc(S.acc, 1)
+    n_acc += 1
+    for d in (1, 2, 3, 4):
+        ve.wait_ge(S["pb%d" % before[d]], quarter)
+        ve.wait_ge(S.acc, n_acc)
+        ve.tensor_tensor(for_me, for_me, blk(T.rxp, 2 * before[d] + 1), add).then_inc(S.acc, 1)
+        n_acc += 1
     ve.wait_ge(S.ss, full)
-    ve.wait_ge(S.acc, 5)
-    ve.tensor_tensor(T.dxs[:], blk(T.ps3, 1), T.rs[:], add).then_inc(S.dxc, 1)
+    ve.wait_ge(S.acc, n_acc)
+    ve.tensor_tensor(T.dxs[:], for_me, T.rs[:], add).then_inc(S.dxc, 1)
 
     sy.wait_ge(S.dxc, 1)
     sy.dma_start(T.dx[:], T.dxs[:]).then_inc(S.stx, 16)
 
-    h0, h1 = helpers[r]
-    f0, f1 = helpers[pr]
+    h0, h1, hb = helpers[r]
+    f0 = helpers[pr][0]
     stay = [e for e in engines(h0) if e not in out]
+    a, b = len(stay) // 2, len(stay) // 2 + len(stay) // 4
     g.wait_ge(S.one, 1)
     g.affine_select(T.idn[:], T.ones[:], [[-1, B]], AluOpType.is_equal, 0.0, 0, 1).then_inc(S.idy, 1)
     g.wait_ge(S.lx, 16)
-    g.remote_dma_fused([transfer(f0, out[:half], S.hpx, T.xs[:], blk(T.hb, 1)),
-                        transfer(f1, out[half:], S.hpx, T.xs[:], blk(T.hb, 1)),
-                        transfer(h0, stay[:len(stay) // 2], S.ho, T.xs[:], blk(T.hb, 0)),
-                        transfer(h1, stay[len(stay) // 2:], S.ho, T.xs[:], blk(T.hb, 0))], local_sem=S.sent)
+    g.remote_dma_fused([transfer(f0, out, S.hpx, T.xs[:], blk(T.hb, 1)),
+                        transfer(h0, stay[:a], S.ho, T.xs[:], blk(T.hb, 0)),
+                        transfer(h1, stay[a:b], S.ho, T.xs[:], blk(T.hb, 0)),
+                        transfer(hb, stay[b:], S.ho, T.xs[:], blk(T.hb, 0))], local_sem=S.sent)
     sent = len(out) + len(stay)
-    mine, sem = blk(T.rxp, 2 * at, 2), S["pw%d" % at]
+    sem = S["pa%d" % at]
     g.wait_ge(S.cs0, 1)
-    sent += two(after[1], after[2], sem, blk(T.stg, 0, 2), blk(T.stg, 2, 2), mine)
+    sent += spread(after[1:5], sem, [blk(T.stg, i) for i in range(4)], blk(T.rxp, 2 * at))
     g.wait_ge(S.cs1, 1)
-    sent += two(after[3], after[4], sem, blk(T.stg, 4, 2), blk(T.stg, 6, 2), mine)
+    sent += write(hb, stay, S.hbb, blk(T.stg, 4, 4), T.bb[:])
     g.wait_ge(S.cs2, 1)
-    sent += write(cores[after[5]], out, sem, blk(T.stg, 8, 2), mine)
+    sent += write(cores[after[5]], out, sem, blk(T.stg, 8, 2), blk(T.rxp, 2 * at, 2))
     g.wait_ge(S.sps, 1)
     sent += write(cores[pr], out, S.ss, T.sp[:], T.rs[:])
     g.wait_ge(S.sent, sent)

from concourse.bass import DstId, RemoteDMATransfer
from concourse.mybir import AluOpType, ActivationFunctionType

B = 128
N = 12
G = 6
WORLD = 512

SCRATCH = {
    "hb": ("sbuf", [128, 2 * B], "bfloat16"),
    "bb": ("sbuf", [128, 4 * B], "bfloat16"),
    "xs": ("sbuf", [128, B], "bfloat16"),
    "wts": ("sbuf", [128, B], "bfloat16"),
    "dys": ("sbuf", [128, N * B], "bfloat16"),
    "dyts": ("sbuf", [128, N * B], "bfloat16"),
    "stg": ("sbuf", [128, 10 * B], "bfloat16"),
    "rxp": ("sbuf", [128, 2 * G * B], "bfloat16"),
    "rxx": ("sbuf", [128, 2 * G * B], "bfloat16"),
    "px": ("sbuf", [128, B], "bfloat16"),
    "sp": ("sbuf", [128, B], "bfloat16"),
    "rs": ("sbuf", [128, B], "bfloat16"),
    "ones": ("sbuf", [128, B], "bfloat16"),
    "idn": ("sbuf", [128, B], "bfloat16"),
    "dxs": ("sbuf", [128, B], "bfloat16"),
    "dws": ("sbuf", [128, B], "bfloat16"),
    "ps0": ("psum", [128, 512], "float32"),
    "ps1": ("psum", [128, 512], "float32"),
    "ps2": ("psum", [128, 512], "float32"),
    "ps3": ("psum", [128, 512], "float32"),
    "psw": ("psum", [128, 512], "float32"),
    "pt0": ("psum", [128, 512], "float32"),
    "pt1": ("psum", [128, 512], "float32"),
    "pt2": ("psum", [128, 512], "float32"),
}
SEMAPHORES = ["lx", "lwt", "lf0", "lf1", "lf2", "one", "idy",
              "mm0", "mm1", "mm2", "mmr", "mmw", "tp0", "tp1", "tp2", "tc0", "tc1", "tc2",
              "cs0", "cs1", "cs2", "acc", "sps", "dxc", "dwc",
              "ho", "hpx", "hp", "hbb", "ss", "xo",
              "pa0", "pa1", "pa2", "pa3", "pa4", "pa5", "pb0", "pb1", "pb2", "pb3", "pb4", "pb5",
              "xw0", "xw1", "xw2", "xw3", "xw4", "xw5",
              "sent", "stx", "stw"]

PLANS = {}


def blk(t, a, n=1):
    return t[:, a * B:(a + n) * B]


def runs_of(ks):
    runs = []
    for k in sorted(ks):
        if runs and runs[-1][0] + runs[-1][1] == k:
            runs[-1][1] += 1
        else:
            runs.append([k, 1])
    return runs


def make_plan(T, topo):
    if "p" in PLANS:
        return PLANS["p"]
    cores = list(T.cores)
    ring, partner, helpers, role = {}, {}, {}, {}
    for q in range(N):
        ring[q] = sorted([q] + [k for k in range(N) if topo.same_plane(cores[q], cores[k])])
        partner[q] = [k for k in range(N) if topo.rack(topo.host(cores[k])) != topo.rack(topo.host(cores[q]))
                      and topo.chip(cores[k]) == topo.chip(cores[q]) and topo.may_write(cores[q], cores[k])][0]
    for q in range(N):
        c = cores[q]
        free = [h for h in range(WORLD) if h not in cores and topo.host(h) == topo.host(c) and topo.chip(h) == topo.chip(c)
                and all(topo.may_write(h, cores[k]) for k in ring[q] if k != q)]
        helpers[q] = ([h for h in free if topo.die(h) != topo.die(c)][0:2]
                      + [h for h in free if topo.die(h) == topo.die(c)][0:1])
        for u in range(3):
            role[helpers[q][u]] = (q, u)
    PLANS["p"] = (ring, partner, helpers, role)
    return PLANS["p"]


def rank_program(g, core, T, topo):
    ring, partner, helpers, role = make_plan(T, topo)
    cores, S = T.cores, T.sem
    add = AluOpType.add

    def engines(dst):
        m = topo.mask(core, dst)
        return [e for e in range(16) if (m >> e) & 1]

    def bits(es):
        return sum(1 << e for e in es)

    def transfer(dst_core, es, sem, src, dst):
        rid, pid = topo.addr(dst_core, core)
        return RemoteDMATransfer(dst_ids=[DstId(rid=rid, pnc=pid)], dma_engine_mask=bits(es), remote_sem=sem, src=src, dst=dst)

    def write(dst_core, es, sem, src, dst):
        rid, pid = topo.addr(dst_core, core)
        g.remote_dma(out_ap=dst, in_ap=src, remote_sem=sem, local_sem=S.sent, pid=pid, routing_id=rid,
                     dma_engine_mask=bits(es))
        return len(es)

    def shares(ks, sem, srcs, dst):
        es = engines(cores[ks[0]])
        w = len(es) // len(ks)
        return [transfer(cores[k], es[i * w:(i + 1) * w], sem, srcs[i], dst) for i, k in enumerate(ks)]

    def spread(ks, sem, srcs, dst):
        g.remote_dma_fused(shares(ks, sem, srcs, dst), local_sem=S.sent)
        return len(engines(cores[ks[0]]))

    if core in role:
        q, u = role[core]
        rg = ring[q]
        at = rg.index(q)
        after = [rg[(at + d) % G] for d in range(G)]
        out = engines(cores[after[1]])
        stay = [e for e in engines(cores[q]) if e not in out]
        o, p = blk(T.hb, 0), blk(T.hb, 1)
        dst_o, dst_p, sem = blk(T.rxx, 2 * at), blk(T.rxx, 2 * at + 1), S["xw%d" % at]
        g.wait_ge(S.ho, len(stay) // 2 if u == 0 else len(stay) // 4)
        if u == 0:
            sent = write(cores[after[1]], out, S.xo, o, dst_o)
            g.wait_ge(S.hpx, len(out))
            inner = stay[:len(stay) // 2]
            g.remote_dma_fused(shares(after[1:5], sem, [p] * 4, dst_p)
                               + [transfer(cores[q], inner, S.hp, p, T.px[:])], local_sem=S.sent)
            sent += len(out) + len(inner)
            sent += write(cores[after[5]], out, sem, p, dst_p)
        elif u == 1:
            sent = spread(after[4:6], S.xo, [o, o], dst_o)
            sent += write(cores[after[2]], out, S.xo, o, dst_o)
        else:
            sent = write(cores[after[3]], out, S.xo, o, dst_o)
            g.wait_ge(S.hbb, len(stay))
            sent += spread(after[1:5], S["pb%d" % at], [blk(T.bb, i) for i in range(4)], blk(T.rxp, 2 * at + 1))
        g.wait_ge(S.sent, sent)
        return

    r = T.rank_of(core)
    if r is None:
        return
    sy, sc, pe, ve = g.sync, g.scalar, g.tensor, g.vector
    pr = partner[r]
    rg = ring[r]
    at = rg.index(r)
    after = [rg[(at + d) % G] for d in range(G)]
    before = [(at - d) % G for d in range(G)]
    out = engines(cores[pr])
    full, half, quarter = len(out), len(out) // 2, len(out) // 4
    order = ([partner[k] for k in after[1:5]] + after[1:5]
             + [partner[after[5]], after[5]])

    def load(queue, ks, sem):
        rs = runs_of(ks)
        for k, n in rs:
            queue.dma_start(blk(T.dys, k, n), blk(T.dy, k, n)).then_inc(sem, 16)
        return 16 * len(rs)

    sy.dma_start(T.xs[:], T.x[:]).then_inc(S.lx, 16)
    n_f0 = load(sc, order[0:4], S.lf0)
    sy.dma_start(T.wts[:], T.wt[:]).then_inc(S.lwt, 16)
    n_f1 = load(sy, order[4:8], S.lf1)
    n_f2 = load(sc, order[8:10] + [pr, r], S.lf2)

    def partials(ks, bank, sem):
        for i, k in enumerate(ks):
            pe.matmul(blk(bank, i), T.wts[:], blk(T.dys, k), True, True).then_inc(sem, 1)

    pe.wait_ge(S.lwt, 16)
    pe.wait_ge(S.lf0, n_f0)
    partials(order[0:4], T.ps0, S.mm0)
    pe.wait_ge(S.lf1, n_f1)
    partials(order[4:8], T.ps1, S.mm1)
    pe.wait_ge(S.lf2, n_f2)
    partials(order[8:10], T.ps2, S.mm2)
    partials([pr, r], T.ps3, S.mmr)
    pe.wait_ge(S.idy, 1)
    for j in range(N):
        pe.matmul(blk(T["pt%d" % (j // 4)], j % 4), blk(T.dys, j), T.idn[:], True, True).then_inc(S["tp%d" % (j // 4)], 1)
    dwp = blk(T.psw, 0)
    pe.wait_ge(S.lx, 16)
    for k in range(3):
        pe.wait_ge(S["tc%d" % k], 1)
    pe.matmul(dwp, T.xs[:], blk(T.dyts, r), True, False)
    pe.wait_ge(S.xo, 3 * full + 2 * half)
    for d in range(1, G):
        pe.matmul(dwp, blk(T.rxx, 2 * before[d]), blk(T.dyts, rg[before[d]]), False, False)
    pe.wait_ge(S.hp, half)
    pe.matmul(dwp, T.px[:], blk(T.dyts, pr), False, False)
    for d in (1, 2, 3, 4):
        pe.wait_ge(S["xw%d" % before[d]], quarter)
        pe.matmul(dwp, blk(T.rxx, 2 * before[d] + 1), blk(T.dyts, partner[rg[before[d]]]), False, False)
    pe.wait_ge(S["xw%d" % before[5]], full)
    pe.matmul(dwp, blk(T.rxx, 2 * before[5] + 1), blk(T.dyts, partner[rg[before[5]]]), False, True).then_inc(S.mmw, 1)

    copy = ActivationFunctionType.Copy
    sc.wait_ge(S.mm1, 4)
    sc.activation(blk(T.stg, 4, 4), T.ps1[:], copy).then_inc(S.cs1, 1)
    for k in range(3):
        sc.wait_ge(S["tp%d" % k], 4)
        sc.activation(blk(T.dyts, 4 * k, 4), T["pt%d" % k][:], copy).then_inc(S["tc%d" % k], 1)
    sc.wait_ge(S.mmw, 1)
    sc.activation(T.dws[:], dwp, copy).then_inc(S.dwc, 1)
    sc.wait_ge(S.dwc, 1)
    sc.dma_start(T.dw[:], T.dws[:]).then_inc(S.stw, 16)

    ve.memset(T.ones[:], 1.0).then_inc(S.one, 1)
    ve.wait_ge(S.mm0, 4)
    ve.tensor_copy(blk(T.stg, 0, 4), blk(T.ps0, 0, 4)).then_inc(S.cs0, 1)
    ve.wait_ge(S.mm2, 2)
    ve.tensor_copy(blk(T.stg, 8, 2), blk(T.ps2, 0, 2)).then_inc(S.cs2, 1)
    ve.wait_ge(S.mmr, 2)
    for_p, for_me = blk(T.ps3, 0), blk(T.ps3, 1)
    n_acc = 0
    for d in (1, 2, 3, 4):
        ve.wait_ge(S["pa%d" % before[d]], quarter)
        if n_acc:
            ve.wait_ge(S.acc, n_acc)
        ve.tensor_tensor(for_p, for_p, blk(T.rxp, 2 * before[d]), add).then_inc(S.acc, 1)
        n_acc += 1
    ve.wait_ge(S["pa%d" % before[5]], full)
    ve.wait_ge(S.acc, n_acc)
    ve.tensor_tensor(T.sp[:], for_p, blk(T.rxp, 2 * before[5]), add).then_inc(S.sps, 1)
    ve.tensor_tensor(for_me, for_me, blk(T.rxp, 2 * before[5] + 1), add).then_inc(S.acc, 1)
    n_acc += 1
    for d in (1, 2, 3, 4):
        ve.wait_ge(S["pb%d" % before[d]], quarter)
        ve.wait_ge(S.acc, n_acc)
        ve.tensor_tensor(for_me, for_me, blk(T.rxp, 2 * before[d] + 1), add).then_inc(S.acc, 1)
        n_acc += 1
    ve.wait_ge(S.ss, full)
    ve.wait_ge(S.acc, n_acc)
    ve.tensor_tensor(T.dxs[:], for_me, T.rs[:], add).then_inc(S.dxc, 1)

    sy.wait_ge(S.dxc, 1)
    sy.dma_start(T.dx[:], T.dxs[:]).then_inc(S.stx, 16)

    h0, h1, hb = helpers[r]
    f0 = helpers[pr][0]
    stay = [e for e in engines(h0) if e not in out]
    a, b = len(stay) // 2, len(stay) // 2 + len(stay) // 4
    g.wait_ge(S.one, 1)
    g.affine_select(T.idn[:], T.ones[:], [[-1, B]], AluOpType.is_equal, 0.0, 0, 1).then_inc(S.idy, 1)
    g.wait_ge(S.lx, 16)
    g.remote_dma_fused([transfer(f0, out, S.hpx, T.xs[:], blk(T.hb, 1)),
                        transfer(h0, stay[:a], S.ho, T.xs[:], blk(T.hb, 0)),
                        transfer(h1, stay[a:b], S.ho, T.xs[:], blk(T.hb, 0)),
                        transfer(hb, stay[b:], S.ho, T.xs[:], blk(T.hb, 0))], local_sem=S.sent)
    sent = len(out) + len(stay)
    sem = S["pa%d" % at]
    g.wait_ge(S.cs0, 1)
    sent += spread(after[1:5], sem, [blk(T.stg, i) for i in range(4)], blk(T.rxp, 2 * at))
    g.wait_ge(S.cs1, 1)
    sent += write(hb, stay, S.hbb, blk(T.stg, 4, 4), T.bb[:])
    g.wait_ge(S.cs2, 1)
    sent += write(cores[after[5]], out, sem, blk(T.stg, 8, 2), blk(T.rxp, 2 * at, 2))
    g.wait_ge(S.sps, 1)
    sent += write(cores[pr], out, S.ss, T.sp[:], T.rs[:])
    g.wait_ge(S.sent, sent)
    g.wait_ge(S.stx, 16)
    g.wait_ge(S.stw, 16)
